import numpy as np
import ml_dtypes


def mxq(x, axis, fmt="e4m3"):
    dtype, down = {"e4m3": (ml_dtypes.float8_e4m3fn, 7), "e5m2": (ml_dtypes.float8_e5m2, 14)}[fmt]
    v = np.moveaxis(np.asarray(x, np.float32).astype(ml_dtypes.bfloat16).astype(np.float64), axis, -1)
    blocks = v.reshape(v.shape[:-1] + (-1, 32))
    amax = np.abs(blocks).max(-1, keepdims=True)
    byte = np.maximum(np.where(amax > 0, np.frexp(amax)[1] - 1 + 127, 0) - down, 1)
    scale = np.exp2(byte - 127.0)
    codes = (blocks / scale).astype(np.float32).astype(dtype).astype(np.float64)
    return np.moveaxis((codes * scale).reshape(v.shape), -1, axis)


WIDE = False


def mx_kscale(k):
    if not WIDE:
        return np.ones(k)
    levels = np.array([10, -10, 5, -5, 0])
    if k % 512:
        return np.exp2(np.random.permutation(np.resize(levels, k // 32))).repeat(32)
    a = np.empty((k // 512, 16))
    for p in range(k // 512):
        a[p, :8] = np.random.permutation(np.resize(levels, 8))
        for g in range(8):
            far = levels[np.abs(levels - a[p, g]) >= 10]
            a[p, g + 8] = far[np.random.randint(len(far))]
    return np.exp2(a.ravel()).repeat(32)


def f64(x):
    return np.asarray(x).astype(np.float64)


def striped(idx):
    return np.tile(idx.reshape(-1, 16).T, (8, 1)).astype(np.uint16)


def unstriped(offs):
    return offs[:16].T.reshape(-1).astype(np.int64)


E2M1 = np.array([0.0, 0.5, 1.0, 1.5, 2.0, 3.0, 4.0, 6.0, -0.0, -0.5, -1.0, -1.5, -2.0, -3.0, -4.0, -6.0])


def pack_weight(w, fmt):
    k, n = w.shape
    w = f64(np.asarray(w, np.float32).astype(ml_dtypes.bfloat16)).reshape(k // 32, 32, n)
    amax = np.abs(w).max(1)
    if fmt == "e4m3":
        byte = np.frexp(amax)[1] - 1 + 127 - 7
    else:
        mant, ex = np.frexp(amax / 6.0)
        byte = np.where(mant > 0.5, ex, ex - 1) + 127
    byte = np.clip(np.where(amax > 0, byte, 1), 1, 254)
    scaled = (w * np.exp2(127.0 - byte)[:, None, :]).reshape(k, n).astype(np.float32)
    by_word = np.ascontiguousarray(scaled.reshape(k // 512, 128, 4, n).transpose(0, 1, 3, 2))
    if fmt == "e4m3":
        words = by_word.astype(ml_dtypes.float8_e4m3fn).view(np.uint8)
    else:
        c = by_word.astype(ml_dtypes.float4_e2m1fn).view(np.uint8) & 0xF
        words = (c[..., 0::2] | (c[..., 1::2] << 4)).reshape(k // 512, 128, 2 * n)
    return np.ascontiguousarray(words), np.ascontiguousarray(byte.astype(np.uint8).reshape(k // 512, 16, n))


def unpack_weight(words, scales, fmt):
    g, _, n = scales.shape
    words = np.ascontiguousarray(words).reshape(g, 128, n, -1)
    if fmt == "e4m3":
        vals = words.view(ml_dtypes.float8_e4m3fn).astype(np.float64)
    else:
        nib = np.empty((g, 128, n, 4), np.uint8)
        nib[..., 0::2] = words & 0xF
        nib[..., 1::2] = words >> 4
        vals = E2M1[nib]
    vals = vals * np.repeat(np.exp2(scales.astype(np.float64) - 127.0), 8, axis=1)[..., None]
    return vals.transpose(0, 1, 3, 2).reshape(g * 512, n)


def gelu(v):
    return 0.5 * v * (1.0 + np.tanh(np.sqrt(2.0 / np.pi) * (v + 0.044715 * v**3)))


K, H, N, T, S, P, P2 = 1024, 1024, 512, 4096, 1024, 512, 256

def setup_inputs():
    n = np.random.standard_normal
    s = mx_kscale(K)[:, None]
    u = mx_kscale(H)[:, None]
    tab_words, tab_scales = pack_weight(n((K, T)) * s, "e4m3")
    w4_words, w4_scales = pack_weight(1.4 / np.sqrt(H) * n((H, N)) / u, "e2m1")
    return {
        "tab_words": tab_words, "tab_scales": tab_scales,
        "offs": striped(np.random.permutation(T)[:S]),
        "pos1": striped(np.random.permutation(S)[:P]),
        "pos2": striped(np.random.permutation(S)[:P]),
        "pos3": striped(np.random.permutation(P)[:P2]),
        "pos4": striped(np.random.permutation(P)[:P2]),
        "w1": (1.5 / np.sqrt(K) * n((K, H)) / s).astype(np.float32),
        "gain": (np.exp(0.3 * n(H)) * u[:, 0]).astype(np.float32),
        "w3": (n((K, N)) / np.sqrt(K) / s).astype(np.float32),
        "w4_words": w4_words, "w4_scales": w4_scales,
    }

def reference(tab_words, tab_scales, offs, pos1, pos2, pos3, pos4, w1, gain, w3, w4_words, w4_scales):
    v = unpack_weight(tab_words, tab_scales, "e4m3")[:, unstriped(offs)]
    w4 = unpack_weight(w4_words, w4_scales, "e2m1")
    l1, l2 = unstriped(pos1), unstriped(pos2)
    a = mxq(f64(w1), 0, "e4m3").T @ v
    gelu = 0.5 * a * (1.0 + np.tanh(0.7978845608028654 * (a + 0.044715 * a ** 3)))
    h = f64(gain)[:, None] * gelu
    sk = mxq(f64(w3), 0, "e4m3").T @ v
    d = np.abs(h[:, l1] - h[:, l2])
    e = w4.T @ mxq(d, 0, "e4m3")
    y = np.tanh(e) * sk[:, l2]
    return np.maximum(y[:, unstriped(pos3)], y[:, unstriped(pos4)])

@@ -1,0 +1,234 @@
+from contextlib import ExitStack
+
+import concourse.mybir as mybir
+
+F32 = mybir.dt.float32
+BF16 = mybir.dt.bfloat16
+I32 = mybir.dt.int32
+U32 = mybir.dt.uint32
+U16 = mybir.dt.uint16
+U8 = mybir.dt.uint8
+FP8X4 = mybir.dt.float8_e4m3fn_x4
+FP4X4 = mybir.dt.float4_e2m1fn_x4
+ACT = mybir.ActivationFunctionType
+ALU = mybir.AluOpType
+
+K, H, N, T, S, R, J = 1024, 1024, 512, 4096, 1024, 512, 256
+FLOPS = 2 * K * H * S + 2 * K * N * S + 2 * H * N * R
+
+P = 128
+PACK = 4
+PASS = P * PACK
+BANK = 512
+QUAD = 32
+
+
+def tile_list_sluice_gate_features_kernel(
+    tc, tab_words, tab_scales, offs, pos1, pos2, pos3, pos4, w1, gain, w3, w4_words, w4_scales, out
+):
+    nc = tc.nc
+    with ExitStack() as ctx:
+        keep = ctx.enter_context(tc.tile_pool(name="keep", bufs=1))
+        psum = ctx.enter_context(tc.psum_pool(name="psum", bufs=8))
+
+        def sb(name, shape, dtype, tag="", bufs=1):
+            return keep.tile(shape, dtype, name=name, tag=tag or name, bufs=bufs, align_bytes=64)
+
+        def load_list(name, src):
+            lst = keep.tile(list(src.shape), U16, name=name)
+            nc.sync.dma_start(lst[:], src)
+            return lst
+
+        tab_sc = sb("tab_sc", [P, T // 4], I32)
+        nc.vector.memset(tab_sc[:], 0)
+        w4_sc = sb("w4_sc", [P, 2, N // 4], I32)
+        nc.vector.memset(w4_sc[:], 0)
+
+        idx = load_list("idx", offs)
+        for q in range(4):
+            nc.scalar.dma_start(
+                out=tab_sc[QUAD * q : QUAD * q + 8, :], in_=tab_scales[:, 4 * q : 4 * q + 4, :].bitcast(I32)
+            )
+        tab_w = []
+        for a in range(2):
+            words = sb("tab_w%d" % a, [P, T], I32)
+            nc.sync.dma_start(out=words[:], in_=tab_words[a].rearrange("p t i -> p (t i)").bitcast(I32))
+            tab_w.append(words)
+
+        def load_weight(name, w, a, c0, width):
+            raw = sb(name, [P, PACK, width], F32)
+            rows = w[a * PASS : (a + 1) * PASS, c0 : c0 + width]
+            nc.sync.dma_start(out=raw[:], in_=rows.rearrange("(p j) c -> p j c", j=PACK))
+            return raw
+
+        half = PASS // 2
+        w1_raw = {}
+        for a in range(2):
+            for u in range(2):
+                w1_raw[0, a, u] = load_weight("w1r0%d%d" % (a, u), w1, a, u * half, half)
+        p1 = load_list("p1", pos1)
+        p2 = load_list("p2", pos2)
+        for a in range(2):
+            for u in range(2):
+                w1_raw[1, a, u] = load_weight("w1r1%d%d" % (a, u), w1, a, PASS + u * half, half)
+        gains = sb("gains", [P, 2, PACK], F32)
+        nc.sync.dma_start(out=gains[:], in_=gain.rearrange("(b p t) -> p b t", b=2, t=PACK))
+        w3_raw = [load_weight("w3r%d" % a, w3, a, 0, N) for a in range(2)]
+        w4_w = sb("w4_w", [P, 2, 2 * N // 4], I32)
+        nc.sync.dma_start(out=w4_w[:], in_=w4_words.rearrange("a p c -> p a c").bitcast(I32))
+        for q in range(4):
+            nc.sync.dma_start(
+                out=w4_sc[QUAD * q : QUAD * q + 4, :, :],
+                in_=w4_scales[:, 4 * q : 4 * q + 4, :].rearrange("a r c -> r a c").bitcast(I32),
+            )
+        p3 = load_list("p3", pos3)
+        p4 = load_list("p4", pos4)
+
+        v_sc = sb("v_sc", [P, S], U8)
+        nc.vector.tensor_copy(v_sc[:], tab_sc[:].bitcast(U8).indirect(idx[:]))
+        v_w = []
+        for a in range(2):
+            picked = sb("v_w%d" % a, [P, S], U32)
+            nc.vector.tensor_copy(picked[:], tab_w[a][:].bitcast(U32).indirect(idx[:]))
+            v_w.append(picked)
+
+        def quantize(name, grouped):
+            codes = sb(name + "c", [P, PASS], U32)
+            scales = sb(name + "s", [P, PASS], U8)
+            nc.vector.quantize_mx(out=codes[:].bitcast(FP8X4), scales=scales[:], in_=grouped[:])
+            return codes, scales
+
+        def weave_w1(b, a, copy):
+            grouped = sb("w1g%d%d" % (b, a), [P, PACK * PASS], BF16, "grouped", 3)
+            dst = grouped[:].rearrange("p (t m j) -> p m j t", t=PACK, j=PACK)
+            for u in range(2):
+                src = w1_raw[b, a, u][:].rearrange("p j (m t) -> p m j t", t=PACK)
+                copy(out=dst[:, u * (P // 2) : (u + 1) * (P // 2), :, :], in_=src)
+            return grouped
+
+        def weave_w3(a, copy):
+            grouped = sb("w3g%d" % a, [P, PACK * N], BF16, "grouped", 3)
+            dst = grouped[:].rearrange("p (c i j) -> p c j i", i=4, j=PACK)
+            src = w3_raw[a][:].rearrange("p j (c i) -> p c j i", i=4)
+            for u in range(2):
+                cols = slice(u * (N // 8), (u + 1) * (N // 8))
+                copy(out=dst[:, cols, :, :], in_=src[:, cols, :, :])
+            return grouped
+
+        def table_pass(acc, weight, col, a, s0):
+            codes, scales = weight
+            nc.tensor.matmul_mx(
+                out=acc[:],
+                lhsT=codes[:, col : col + P].bitcast(FP8X4),
+                lhsT_scale=scales[:, col : col + P],
+                rhs=v_w[a][:, s0 : s0 + BANK].bitcast(FP8X4),
+                rhs_scale=v_sc[4 * a : P, s0 : s0 + BANK],
+                start=(a == 0),
+                stop=(a == 1),
+            )
+
+        def bank():
+            return psum.tile([P, BANK], F32, name="acc")
+
+        def gelu_rows(b, t, accs):
+            g = sb("g%d%d" % (b, t), [P, S], F32, "page", 6)
+            for s in range(2):
+                nc.scalar.activation(out=g[:, s * BANK : (s + 1) * BANK], in_=accs[s][:], func=ACT.Gelu_apprx_tanh)
+            return g
+
+        def product(weight, col):
+            accs = [bank(), bank()]
+            for s in range(2):
+                for a in range(2):
+                    table_pass(accs[s], weight[a], col, a, s * BANK)
+            return accs
+
+        def difference(b, t, g):
+            up = sb("up%d%d" % (b, t), [P, R], F32, "up", 2)
+            diff = sb("diff%d%d" % (b, t), [P, R], F32)
+            nc.vector.tensor_copy(up[:], g[:].indirect(p1[:]))
+            nc.vector.tensor_tensor(diff[:], g[:].indirect(p2[:]), up[:], ALU.subtract)
+            return diff
+
+        def round_abs(b, t, diff, rows):
+            nc.scalar.activation(out=rows[:, t, :], in_=diff[:], func=ACT.Abs, scale=gains[:, b, t : t + 1])
+
+        def weave_d(b, rows, copy):
+            grouped = sb("dg%d" % b, [P, PACK * R], BF16, "grouped", 3)
+            copy(
+                out=grouped[:].rearrange("p (c i t) -> p c t i", i=4, t=PACK),
+                in_=rows[:].rearrange("p t (c i) -> p c t i", i=4),
+            )
+            return grouped
+
+        w1q = {}
+        w1q[0, 0] = quantize("w1q00", weave_w1(0, 0, nc.vector.tensor_copy))
+        accs0 = [[bank(), bank()] for t in range(PACK)]
+        for t in range(PACK):
+            for s in range(2):
+                table_pass(accs0[t][s], w1q[0, 0], t * P, 0, s * BANK)
+        w1q[0, 1] = quantize("w1q01", weave_w1(0, 1, nc.vector.tensor_copy))
+        for t in range(PACK):
+            for s in range(2):
+                table_pass(accs0[t][s], w1q[0, 1], t * P, 1, s * BANK)
+
+        d_rows = [sb("drows%d" % b, [P, PACK, R], BF16) for b in range(2)]
+        diffs = {}
+        gs = {}
+        gs[0] = gelu_rows(0, 0, accs0[0])
+        gs[1] = gelu_rows(0, 1, accs0[1])
+        diffs[0, 0] = difference(0, 0, gs[0])
+        g10 = weave_w1(1, 0, nc.scalar.copy)
+        gs[2] = gelu_rows(0, 2, accs0[2])
+        diffs[0, 1] = difference(0, 1, gs[1])
+        w1q[1, 0] = quantize("w1q10", g10)
+        gs[3] = gelu_rows(0, 3, accs0[3])
+        g11 = weave_w1(1, 1, nc.scalar.copy)
+        diffs[0, 2] = difference(0, 2, gs[2])
+        w1q[1, 1] = quantize("w1q11", g11)
+        diffs[0, 3] = difference(0, 3, gs[3])
+
+        w3g = {}
+        for t in range(PACK):
+            g = gelu_rows(1, t, product([w1q[1, 0], w1q[1, 1]], t * P))
+            if t % 2 == 1:
+                w3g[t // 2] = weave_w3(t // 2, nc.scalar.copy)
+            diffs[1, t] = difference(1, t, g)
+            round_abs(0, t, diffs[0, t], d_rows[0])
+        w3q = [quantize("w3q%d" % a, w3g[a]) for a in range(2)]
+        dq = [quantize("dq0", weave_d(0, d_rows[0], nc.scalar.copy))]
+        for t in range(PACK):
+            round_abs(1, t, diffs[1, t], d_rows[1])
+        dq.append(quantize("dq1", weave_d(1, d_rows[1], nc.vector.tensor_copy)))
+
+        sks = []
+        for n in range(N // P):
+            accs = product(w3q, n * P)
+            sk = sb("sk%d" % n, [P, S], F32, "page", 6)
+            for s in range(2):
+                nc.scalar.copy(out=sk[:, s * BANK : (s + 1) * BANK], in_=accs[s][:])
+            sks.append(sk)
+
+        for n in range(N // P):
+            acc = bank()
+            for b in range(2):
+                codes, scales = dq[b]
+                nc.tensor.matmul_mx(
+                    out=acc[:],
+                    lhsT=w4_w[:, b, :].bitcast(U8)[:, 2 * n * P : 2 * (n + 1) * P].bitcast(FP4X4),
+                    lhsT_scale=w4_sc[:, b, :].bitcast(U8)[:, n * P : (n + 1) * P],
+                    rhs=codes[:].bitcast(FP8X4),
+                    rhs_scale=scales[:],
+                    start=(b == 0),
+                    stop=(b == 1),
+                )
+            gate = sb("gate%d" % n, [P, R], F32)
+            nc.scalar.activation(out=gate[:], in_=acc[:], func=ACT.Tanh)
+            y = sb("y%d" % n, [P, R], F32)
+            nc.vector.tensor_tensor(y[:], sks[n][:].indirect(p2[:]), gate[:], ALU.mult)
+            pair = sb("pair%d" % n, [P, 2, J], F32)
+            nc.vector.tensor_copy(pair[:, 0, :], y[:].indirect(p3[:]))
+            nc.vector.tensor_copy(pair[:, 1, :], y[:].indirect(p4[:]))
+            best = sb("best%d" % n, [P, J], F32)
+            nc.vector.tensor_tensor(best[:], pair[:, 0, :], pair[:, 1, :], ALU.max)
+            nc.sync.dma_start(out=out[n * P : (n + 1) * P, :], in_=best[:])

@@ -29,7 +29,7 @@ def tile_list_sluice_gate_features_kernel(
     nc = tc.nc
     with ExitStack() as ctx:
         keep = ctx.enter_context(tc.tile_pool(name="keep", bufs=1))
-        psum = ctx.enter_context(tc.psum_pool(name="psum", bufs=8))
+        psum = ctx.enter_context(tc.psum_pool(name="psum", bufs=1))
 
         def sb(name, shape, dtype, tag="", bufs=1):
             return keep.tile(shape, dtype, name=name, tag=tag or name, bufs=bufs, align_bytes=64)
@@ -39,21 +39,21 @@ def tile_list_sluice_gate_features_kernel(
             nc.sync.dma_start(lst[:], src)
             return lst
 
-        tab_sc = sb("tab_sc", [P, T // 4], I32)
+        tab_sc = sb("tab_sc", [P, T // 4], I32, "sc_then_w1")
         nc.vector.memset(tab_sc[:], 0)
+        for q in range(4):
+            nc.gpsimd.dma_start(
+                out=tab_sc[QUAD * q : QUAD * q + 8, :], in_=tab_scales[:, 4 * q : 4 * q + 4, :].bitcast(I32)
+            )
         w4_sc = sb("w4_sc", [P, 2, N // 4], I32)
         nc.vector.memset(w4_sc[:], 0)
 
         idx = load_list("idx", offs)
-        for q in range(4):
-            nc.scalar.dma_start(
-                out=tab_sc[QUAD * q : QUAD * q + 8, :], in_=tab_scales[:, 4 * q : 4 * q + 4, :].bitcast(I32)
-            )
-        tab_w = []
-        for a in range(2):
-            words = sb("tab_w%d" % a, [P, T], I32)
+
+        def load_table(a):
+            words = sb("tab_w%d" % a, [P, T], I32, "tab%d" % a)
             nc.sync.dma_start(out=words[:], in_=tab_words[a].rearrange("p t i -> p (t i)").bitcast(I32))
-            tab_w.append(words)
+            return words
 
         def load_weight(name, w, a, c0, width):
             raw = sb(name, [P, PACK, width], F32)
@@ -63,14 +63,14 @@ def tile_list_sluice_gate_features_kernel(
 
         half = PASS // 2
         w1_raw = {}
-        for a in range(2):
-            for u in range(2):
-                w1_raw[0, a, u] = load_weight("w1r0%d%d" % (a, u), w1, a, u * half, half)
+        tab_w = [load_table(0)]
+        w1_raw[0, 0] = [load_weight("w1r00", w1, 0, 0, PASS)]
+        tab_w.append(load_table(1))
+        w1_raw[0, 1] = [load_weight("w1r01", w1, 1, 0, PASS)]
         p1 = load_list("p1", pos1)
         p2 = load_list("p2", pos2)
         for a in range(2):
-            for u in range(2):
-                w1_raw[1, a, u] = load_weight("w1r1%d%d" % (a, u), w1, a, PASS + u * half, half)
+            w1_raw[1, a] = [load_weight("w1r1%d" % a, w1, a, PASS, PASS)]
         gains = sb("gains", [P, 2, PACK], F32)
         nc.sync.dma_start(out=gains[:], in_=gain.rearrange("(b p t) -> p b t", b=2, t=PACK))
         w3_raw = [load_weight("w3r%d" % a, w3, a, 0, N) for a in range(2)]
@@ -87,32 +87,42 @@ def tile_list_sluice_gate_features_kernel(
         v_sc = sb("v_sc", [P, S], U8)
         nc.vector.tensor_copy(v_sc[:], tab_sc[:].bitcast(U8).indirect(idx[:]))
         v_w = []
-        for a in range(2):
-            picked = sb("v_w%d" % a, [P, S], U32)
+
+        def pick_words(a, tag):
+            picked = sb("v_w%d" % a, [P, S], U32, tag)
             nc.vector.tensor_copy(picked[:], tab_w[a][:].bitcast(U32).indirect(idx[:]))
             v_w.append(picked)
 
-        def quantize(name, grouped):
-            codes = sb(name + "c", [P, PASS], U32)
-            scales = sb(name + "s", [P, PASS], U8)
-            nc.vector.quantize_mx(out=codes[:].bitcast(FP8X4), scales=scales[:], in_=grouped[:])
+        def quantize(name, grouped, parts=1, tag=""):
+            width = grouped.shape[1] // PACK
+            codes = sb(name + "c", [P, width], U32, tag)
+            scales = sb(name + "s", [P, width], U8)
+            step = width // parts
+            for c in range(0, width, step):
+                quantize_cols(codes, scales, grouped, c, step)
             return codes, scales
 
-        def weave_w1(b, a, copy):
-            grouped = sb("w1g%d%d" % (b, a), [P, PACK * PASS], BF16, "grouped", 3)
+        def quantize_cols(codes, scales, grouped, c, step):
+            nc.vector.quantize_mx(
+                out=codes[:, c : c + step].bitcast(FP8X4),
+                scales=scales[:, c : c + step],
+                in_=grouped[:, PACK * c : PACK * (c + step)],
+            )
+
+        def weave_w1(b, a, copy, grouped):
             dst = grouped[:].rearrange("p (t m j) -> p m j t", t=PACK, j=PACK)
-            for u in range(2):
-                src = w1_raw[b, a, u][:].rearrange("p j (m t) -> p m j t", t=PACK)
-                copy(out=dst[:, u * (P // 2) : (u + 1) * (P // 2), :, :], in_=src)
+            m0 = 0
+            for raw in w1_raw[b, a]:
+                src = raw[:].rearrange("p j (m t) -> p m j t", t=PACK)
+                copy(out=dst[:, m0 : m0 + src.shape[1], :, :], in_=src)
+                m0 = m0 + src.shape[1]
             return grouped
 
-        def weave_w3(a, copy):
-            grouped = sb("w3g%d" % a, [P, PACK * N], BF16, "grouped", 3)
-            dst = grouped[:].rearrange("p (c i j) -> p c j i", i=4, j=PACK)
-            src = w3_raw[a][:].rearrange("p j (c i) -> p c j i", i=4)
-            for u in range(2):
-                cols = slice(u * (N // 8), (u + 1) * (N // 8))
-                copy(out=dst[:, cols, :, :], in_=src[:, cols, :, :])
+        def weave_w3(a, copy, grouped):
+            copy(
+                out=grouped[:].rearrange("p (c i j) -> p c j i", i=4, j=PACK),
+                in_=w3_raw[a][:].rearrange("p j (c i) -> p c j i", i=4),
+            )
             return grouped
 
         def table_pass(acc, weight, col, a, s0):
@@ -127,8 +137,8 @@ def tile_list_sluice_gate_features_kernel(
                 stop=(a == 1),
             )
 
-        def bank():
-            return psum.tile([P, BANK], F32, name="acc")
+        def bank(tag="wide"):
+            return psum.tile([P, BANK], F32, name="acc", tag=tag, bufs=6 if tag == "wide" else 2)
 
         def gelu_rows(b, t, accs):
             g = sb("g%d%d" % (b, t), [P, S], F32, "page", 6)
@@ -143,92 +153,122 @@ def tile_list_sluice_gate_features_kernel(
                     table_pass(accs[s], weight[a], col, a, s * BANK)
             return accs
 
-        def difference(b, t, g):
-            up = sb("up%d%d" % (b, t), [P, R], F32, "up", 2)
-            diff = sb("diff%d%d" % (b, t), [P, R], F32)
-            nc.vector.tensor_copy(up[:], g[:].indirect(p1[:]))
-            nc.vector.tensor_tensor(diff[:], g[:].indirect(p2[:]), up[:], ALU.subtract)
-            return diff
+        def difference(diff, g, up, m0=0, width=R):
+            cols = slice(m0, m0 + width)
+            lst = slice(m0 // 16, (m0 + width) // 16)
+            nc.vector.tensor_copy(up[:, cols], g[:].indirect(p1[:, lst]))
+            nc.vector.tensor_tensor(diff[:, cols], g[:].indirect(p2[:, lst]), up[:, cols], ALU.subtract)
 
-        def round_abs(b, t, diff, rows):
-            nc.scalar.activation(out=rows[:, t, :], in_=diff[:], func=ACT.Abs, scale=gains[:, b, t : t + 1])
-
-        def weave_d(b, rows, copy):
-            grouped = sb("dg%d" % b, [P, PACK * R], BF16, "grouped", 3)
-            copy(
-                out=grouped[:].rearrange("p (c i t) -> p c t i", i=4, t=PACK),
-                in_=rows[:].rearrange("p t (c i) -> p c t i", i=4),
+        def round_abs(b, t, m0=0, width=R):
+            cols = slice(m0, m0 + width)
+            nc.scalar.activation(
+                out=d_rows[b][:, t, cols], in_=diffs[b, t][:, cols], func=ACT.Abs, scale=gains[:, b, t : t + 1]
             )
-            return grouped
 
-        w1q = {}
-        w1q[0, 0] = quantize("w1q00", weave_w1(0, 0, nc.vector.tensor_copy))
-        accs0 = [[bank(), bank()] for t in range(PACK)]
-        for t in range(PACK):
-            for s in range(2):
-                table_pass(accs0[t][s], w1q[0, 0], t * P, 0, s * BANK)
-        w1q[0, 1] = quantize("w1q01", weave_w1(0, 1, nc.vector.tensor_copy))
-        for t in range(PACK):
-            for s in range(2):
-                table_pass(accs0[t][s], w1q[0, 1], t * P, 1, s * BANK)
+        def weave_d(b, grouped, copy, m0=0, width=R):
+            copy(
+                out=grouped[:, PACK * m0 : PACK * (m0 + width)].rearrange("p (c i t) -> p c t i", i=4, t=PACK),
+                in_=d_rows[b][:, :, m0 : m0 + width].rearrange("p t (c i) -> p c t i", i=4),
+            )
 
-        d_rows = [sb("drows%d" % b, [P, PACK, R], BF16) for b in range(2)]
-        diffs = {}
-        gs = {}
-        gs[0] = gelu_rows(0, 0, accs0[0])
-        gs[1] = gelu_rows(0, 1, accs0[1])
-        diffs[0, 0] = difference(0, 0, gs[0])
-        g10 = weave_w1(1, 0, nc.scalar.copy)
-        gs[2] = gelu_rows(0, 2, accs0[2])
-        diffs[0, 1] = difference(0, 1, gs[1])
-        w1q[1, 0] = quantize("w1q10", g10)
-        gs[3] = gelu_rows(0, 3, accs0[3])
-        g11 = weave_w1(1, 1, nc.scalar.copy)
-        diffs[0, 2] = difference(0, 2, gs[2])
-        w1q[1, 1] = quantize("w1q11", g11)
-        diffs[0, 3] = difference(0, 3, gs[3])
-
-        w3g = {}
-        for t in range(PACK):
-            g = gelu_rows(1, t, product([w1q[1, 0], w1q[1, 1]], t * P))
-            if t % 2 == 1:
-                w3g[t // 2] = weave_w3(t // 2, nc.scalar.copy)
-            diffs[1, t] = difference(1, t, g)
-            round_abs(0, t, diffs[0, t], d_rows[0])
-        w3q = [quantize("w3q%d" % a, w3g[a]) for a in range(2)]
-        dq = [quantize("dq0", weave_d(0, d_rows[0], nc.scalar.copy))]
-        for t in range(PACK):
-            round_abs(1, t, diffs[1, t], d_rows[1])
-        dq.append(quantize("dq1", weave_d(1, d_rows[1], nc.vector.tensor_copy)))
-
-        sks = []
-        for n in range(N // P):
+        def skip_rows(n, copies):
             accs = product(w3q, n * P)
             sk = sb("sk%d" % n, [P, S], F32, "page", 6)
             for s in range(2):
-                nc.scalar.copy(out=sk[:, s * BANK : (s + 1) * BANK], in_=accs[s][:])
-            sks.append(sk)
+                copies[s](out=sk[:, s * BANK : (s + 1) * BANK], in_=accs[s][:])
+            return sk
 
-        for n in range(N // P):
-            acc = bank()
+        def gated(n, sk, y, m0, width):
+            cols = slice(m0, m0 + width)
+            acc = bank("gate")
             for b in range(2):
                 codes, scales = dq[b]
                 nc.tensor.matmul_mx(
-                    out=acc[:],
+                    out=acc[:, 0:width],
                     lhsT=w4_w[:, b, :].bitcast(U8)[:, 2 * n * P : 2 * (n + 1) * P].bitcast(FP4X4),
                     lhsT_scale=w4_sc[:, b, :].bitcast(U8)[:, n * P : (n + 1) * P],
-                    rhs=codes[:].bitcast(FP8X4),
-                    rhs_scale=scales[:],
+                    rhs=codes[:, cols].bitcast(FP8X4),
+                    rhs_scale=scales[:, cols],
                     start=(b == 0),
                     stop=(b == 1),
                 )
-            gate = sb("gate%d" % n, [P, R], F32)
-            nc.scalar.activation(out=gate[:], in_=acc[:], func=ACT.Tanh)
-            y = sb("y%d" % n, [P, R], F32)
-            nc.vector.tensor_tensor(y[:], sks[n][:].indirect(p2[:]), gate[:], ALU.mult)
+            gate = sb("gate%d_%d" % (n, m0), [P, width], F32)
+            nc.scalar.activation(out=gate[:], in_=acc[:, 0:width], func=ACT.Tanh)
+            lst = slice(m0 // 16, (m0 + width) // 16)
+            nc.vector.tensor_tensor(y[:, cols], sk[:].indirect(p2[:, lst]), gate[:], ALU.mult)
+
+        def finish(n, y):
             pair = sb("pair%d" % n, [P, 2, J], F32)
             nc.vector.tensor_copy(pair[:, 0, :], y[:].indirect(p3[:]))
             nc.vector.tensor_copy(pair[:, 1, :], y[:].indirect(p4[:]))
             best = sb("best%d" % n, [P, J], F32)
             nc.vector.tensor_tensor(best[:], pair[:, 0, :], pair[:, 1, :], ALU.max)
             nc.sync.dma_start(out=out[n * P : (n + 1) * P, :], in_=best[:])
+
+        on_v, on_s = nc.vector.tensor_copy, nc.scalar.copy
+
+        def staged(name, tag=""):
+            return sb(name, [P, PACK * PASS], BF16, tag)
+
+        def two(pair):
+            codes, scales = pair
+            return [(codes[:, a * PASS : (a + 1) * PASS], scales[:, a * PASS : (a + 1) * PASS]) for a in range(2)]
+
+        pick_words(0, "sc_then_w1")
+        w1q = {}
+        w1q[0, 0] = quantize("w1q00", weave_w1(0, 0, on_s, staged("w1g00")), 1, "tab0")
+        accs0 = [[bank("wide" if t < 3 else "gate") for s in range(2)] for t in range(PACK)]
+        for t in range(PACK):
+            for s in range(2):
+                table_pass(accs0[t][s], w1q[0, 0], t * P, 0, s * BANK)
+        pick_words(1, "w1g00")
+        w1q[0, 1] = quantize("w1q01", weave_w1(0, 1, on_v, staged("w1g01", "tab1")), 2)
+        for t in range(PACK):
+            for s in range(2):
+                table_pass(accs0[t][s], w1q[0, 1], t * P, 1, s * BANK)
+
+        d_rows = [sb("drows%d" % b, [P, PACK, R], BF16) for b in range(2)]
+        diffs = {(b, t): sb("diff%d%d" % (b, t), [P, R], F32) for b in range(2) for t in range(PACK)}
+        shared = [sb("shared%d" % u, [P, 4 * R], F32) for u in range(2)]
+        ups = [shared[t // 2][:, 2 * R * (t % 2) : 2 * R * (t % 2) + R] for t in range(PACK)]
+        stage = [shared[t // 2][:, 2 * R * (t % 2) : 2 * R * (t % 2 + 1)].bitcast(BF16) for t in range(PACK)]
+        gs = [gelu_rows(0, t, accs0[t]) for t in range(3)]
+        for t in range(3):
+            difference(diffs[0, t], gs[t], ups[t])
+        for a in range(2):
+            weave_w1(1, a, on_s, stage[a])
+        w1q1 = two(quantize("w1q1", shared[0][:].bitcast(BF16)))
+        difference(diffs[0, 3], gelu_rows(0, 3, accs0[3]), ups[3])
+        for t in range(PACK):
+            g = gelu_rows(1, t, product(w1q1, t * P))
+            up = sb("up1%d" % t, [P, R], F32, "up", 2)
+            if t < 3:
+                difference(diffs[1, t], g, up)
+            else:
+                for m0 in (0, half):
+                    difference(diffs[1, t], g, up, m0, half)
+            if t in (1, 2):
+                weave_w3(t - 1, on_s, stage[t + 1])
+        w3q = two(quantize("w3q", shared[1][:].bitcast(BF16)))
+        dg = [staged("dg%d" % b) for b in range(2)]
+        for t in range(PACK):
+            round_abs(0, t)
+        weave_d(0, dg[0], on_s)
+        dq = [quantize("dq0", dg[0])]
+        for t in range(3):
+            round_abs(1, t)
+        dq.append((sb("dq1c", [P, R], U32), sb("dq1s", [P, R], U8)))
+        for m0 in (0, half):
+            round_abs(1, 3, m0, half)
+            weave_d(1, dg[1], on_v, m0, half)
+        for m0 in (0, half):
+            quantize_cols(dq[1][0], dq[1][1], dg[1], m0, half)
+        for n in range(N // P):
+            sk = skip_rows(n, [on_s, on_s])
+            y = sb("y%d" % n, [P, R], F32)
+            if n == 0:
+                for m0 in (0, half):
+                    gated(n, sk, y, m0, half)
+            else:
+                gated(n, sk, y, 0, R)
+            finish(n, y)

@@ -29,6 +29,7 @@ def tile_list_sluice_gate_features_kernel(
     nc = tc.nc
     with ExitStack() as ctx:
         keep = ctx.enter_context(tc.tile_pool(name="keep", bufs=1))
+        reuse = ctx.enter_context(tc.tile_pool(name="reuse", bufs=1))
         psum = ctx.enter_context(tc.psum_pool(name="psum", bufs=1))
 
         def sb(name, shape, dtype, tag="", bufs=1):
@@ -39,7 +40,7 @@ def tile_list_sluice_gate_features_kernel(
             nc.sync.dma_start(lst[:], src)
             return lst
 
-        tab_sc = sb("tab_sc", [P, T // 4], I32, "sc_then_w1")
+        tab_sc = sb("tab_sc", [P, T // 4], I32)
         nc.vector.memset(tab_sc[:], 0)
         for q in range(4):
             nc.gpsimd.dma_start(
@@ -48,10 +49,9 @@ def tile_list_sluice_gate_features_kernel(
         w4_sc = sb("w4_sc", [P, 2, N // 4], I32)
         nc.vector.memset(w4_sc[:], 0)
 
-        idx = load_list("idx", offs)
 
         def load_table(a):
-            words = sb("tab_w%d" % a, [P, T], I32, "tab%d" % a)
+            words = sb("tab_w%d" % a, [P, T], I32)
             nc.sync.dma_start(out=words[:], in_=tab_words[a].rearrange("p t i -> p (t i)").bitcast(I32))
             return words
 
@@ -64,9 +64,10 @@ def tile_list_sluice_gate_features_kernel(
         half = PASS // 2
         w1_raw = {}
         tab_w = [load_table(0)]
+        idx = load_list("idx", offs)
         w1_raw[0, 0] = [load_weight("w1r00", w1, 0, 0, PASS)]
         tab_w.append(load_table(1))
-        w1_raw[0, 1] = [load_weight("w1r01", w1, 1, 0, PASS)]
+        w1_raw[0, 1] = [load_weight("w1r01%d" % u, w1, 1, u * half, half) for u in range(2)]
         p1 = load_list("p1", pos1)
         p2 = load_list("p2", pos2)
         for a in range(2):
@@ -84,8 +85,6 @@ def tile_list_sluice_gate_features_kernel(
         p3 = load_list("p3", pos3)
         p4 = load_list("p4", pos4)
 
-        v_sc = sb("v_sc", [P, S], U8)
-        nc.vector.tensor_copy(v_sc[:], tab_sc[:].bitcast(U8).indirect(idx[:]))
         v_w = []
 
         def pick_words(a, tag):
@@ -109,21 +108,19 @@ def tile_list_sluice_gate_features_kernel(
                 in_=grouped[:, PACK * c : PACK * (c + step)],
             )
 
-        def weave_w1(b, a, copy, grouped):
+        def weave_w1(raw, copy, grouped, t0=0, t1=PACK):
             dst = grouped[:].rearrange("p (t m j) -> p m j t", t=PACK, j=PACK)
-            m0 = 0
-            for raw in w1_raw[b, a]:
-                src = raw[:].rearrange("p j (m t) -> p m j t", t=PACK)
-                copy(out=dst[:, m0 : m0 + src.shape[1], :, :], in_=src)
-                m0 = m0 + src.shape[1]
-            return grouped
+            src = raw[:].rearrange("p j (m t) -> p m j t", t=PACK)
+            copy(out=dst[:, :, :, t0:t1], in_=src[:, :, :, t0:t1])
 
-        def weave_w3(a, copy, grouped):
+        def weave_w3(u, a, copy, grouped):
             copy(
-                out=grouped[:].rearrange("p (c i j) -> p c j i", i=4, j=PACK),
-                in_=w3_raw[a][:].rearrange("p j (c i) -> p c j i", i=4),
+                out=grouped.rearrange("p (c i j) -> p c j i", i=4, j=PACK),
+                in_=w3_raw[a][:, :, u * half : (u + 1) * half].rearrange("p j (c i) -> p c j i", i=4),
             )
             return grouped
+
+        banks = []
 
         def table_pass(acc, weight, col, a, s0):
             codes, scales = weight
@@ -137,8 +134,10 @@ def tile_list_sluice_gate_features_kernel(
                 stop=(a == 1),
             )
 
-        def bank(tag="wide"):
-            return psum.tile([P, BANK], F32, name="acc", tag=tag, bufs=6 if tag == "wide" else 2)
+        def bank(index):
+            name = "acc%d" % len(banks)
+            banks.append(psum.tile([P, BANK], F32, name=name, offset=4 * BANK * index))
+            return banks[-1]
 
         def gelu_rows(b, t, accs):
             g = sb("g%d%d" % (b, t), [P, S], F32, "page", 6)
@@ -146,18 +145,19 @@ def tile_list_sluice_gate_features_kernel(
                 nc.scalar.activation(out=g[:, s * BANK : (s + 1) * BANK], in_=accs[s][:], func=ACT.Gelu_apprx_tanh)
             return g
 
-        def product(weight, col):
-            accs = [bank(), bank()]
-            for s in range(2):
-                for a in range(2):
+        def product(weight, col, first):
+            accs = [bank(first), bank(first + 1)]
+            for a in range(2):
+                for s in range(2):
                     table_pass(accs[s], weight[a], col, a, s * BANK)
             return accs
 
-        def difference(diff, g, up, m0=0, width=R):
-            cols = slice(m0, m0 + width)
-            lst = slice(m0 // 16, (m0 + width) // 16)
-            nc.vector.tensor_copy(up[:, cols], g[:].indirect(p1[:, lst]))
-            nc.vector.tensor_tensor(diff[:, cols], g[:].indirect(p2[:, lst]), up[:, cols], ALU.subtract)
+        def difference(diff, g, up):
+            parts = [(slice(m0, m0 + half), slice(m0 // 16, (m0 + half) // 16)) for m0 in (0, half)]
+            for cols, lst in parts:
+                nc.vector.tensor_copy(up[:, cols], g[:].indirect(p1[:, lst]))
+            for cols, lst in parts:
+                nc.vector.tensor_tensor(diff[:, cols], g[:].indirect(p2[:, lst]), up[:, cols], ALU.subtract)
 
         def round_abs(b, t, m0=0, width=R):
             cols = slice(m0, m0 + width)
@@ -172,7 +172,7 @@ def tile_list_sluice_gate_features_kernel(
             )
 
         def skip_rows(n, copies):
-            accs = product(w3q, n * P)
+            accs = product(w3q[n // 2], (n % 2) * P, (6, 2)[n % 2])
             sk = sb("sk%d" % n, [P, S], F32, "page", 6)
             for s in range(2):
                 copies[s](out=sk[:, s * BANK : (s + 1) * BANK], in_=accs[s][:])
@@ -180,7 +180,7 @@ def tile_list_sluice_gate_features_kernel(
 
         def gated(n, sk, y, m0, width):
             cols = slice(m0, m0 + width)
-            acc = bank("gate")
+            acc = bank((4 + m0 // half, 0, 6, 7)[n])
             for b in range(2):
                 codes, scales = dq[b]
                 nc.tensor.matmul_mx(
@@ -212,49 +212,65 @@ def tile_list_sluice_gate_features_kernel(
 
         def two(pair):
             codes, scales = pair
-            return [(codes[:, a * PASS : (a + 1) * PASS], scales[:, a * PASS : (a + 1) * PASS]) for a in range(2)]
+            w = codes.shape[1] // 2
+            return [(codes[:, a * w : (a + 1) * w], scales[:, a * w : (a + 1) * w]) for a in range(2)]
 
-        pick_words(0, "sc_then_w1")
+        pick_words(0, "")
         w1q = {}
-        w1q[0, 0] = quantize("w1q00", weave_w1(0, 0, on_s, staged("w1g00")), 1, "tab0")
-        accs0 = [[bank("wide" if t < 3 else "gate") for s in range(2)] for t in range(PACK)]
-        for t in range(PACK):
+        stage00 = reuse.tile([P, PACK * PASS], BF16, name="w1g00", offset=0, align_bytes=64)
+        weave_w1(w1_raw[0, 0][0], on_s, stage00, 2, 4)
+        weave_w1(w1_raw[0, 0][0], on_v, stage00, 0, 2)
+        w1q[0, 0] = quantize("w1q00", stage00)
+        v_sc = reuse.tile([P, S], U8, name="v_sc", offset=0, align_bytes=64)
+        nc.vector.tensor_copy(v_sc[:], tab_sc[:].bitcast(U8).indirect(idx[:]))
+        accs0 = [[bank(2 * t + s) for s in range(2)] for t in range(3)]
+        for t in range(3):
             for s in range(2):
                 table_pass(accs0[t][s], w1q[0, 0], t * P, 0, s * BANK)
-        pick_words(1, "w1g00")
-        w1q[0, 1] = quantize("w1q01", weave_w1(0, 1, on_v, staged("w1g01", "tab1")), 2)
+        pick_words(1, "")
+        w1q[0, 1] = (sb("w1q01c", [P, PASS], U32), sb("w1q01s", [P, PASS], U8))
+        parts = [sb("w1g01%d" % u, [P, PACK * half], BF16) for u in range(2)]
+        for u in range(2):
+            weave_w1(w1_raw[0, 1][u], [on_s, on_v][u], parts[u])
         for t in range(PACK):
+            for u in (1, 0):
+                cols = slice(t * P + u * (P // 2), t * P + (u + 1) * (P // 2))
+                nc.vector.quantize_mx(
+                    out=w1q[0, 1][0][:, cols].bitcast(FP8X4),
+                    scales=w1q[0, 1][1][:, cols],
+                    in_=parts[u][:, t * half : (t + 1) * half],
+                )
+        for t in range(3):
             for s in range(2):
                 table_pass(accs0[t][s], w1q[0, 1], t * P, 1, s * BANK)
 
         d_rows = [sb("drows%d" % b, [P, PACK, R], BF16) for b in range(2)]
         diffs = {(b, t): sb("diff%d%d" % (b, t), [P, R], F32) for b in range(2) for t in range(PACK)}
-        shared = [sb("shared%d" % u, [P, 4 * R], F32) for u in range(2)]
-        ups = [shared[t // 2][:, 2 * R * (t % 2) : 2 * R * (t % 2) + R] for t in range(PACK)]
-        stage = [shared[t // 2][:, 2 * R * (t % 2) : 2 * R * (t % 2 + 1)].bitcast(BF16) for t in range(PACK)]
+        shared = [sb("shared0", [P, 4 * R], F32), sb("shared1", [P, 2 * R], F32)]
+        ups = [sb("up0%d" % t, [P, R], F32, "up", 2) for t in range(PACK)]
+        ups[0] = shared[0][:, 3 * half : 5 * half]
+        ups[2] = shared[1][:, half : 3 * half]
         gs = [gelu_rows(0, t, accs0[t]) for t in range(3)]
         for t in range(3):
             difference(diffs[0, t], gs[t], ups[t])
         for a in range(2):
-            weave_w1(1, a, on_s, stage[a])
+            weave_w1(w1_raw[1, a][0], on_s, shared[0][:, 2 * R * a : 2 * R * (a + 1)].bitcast(BF16))
         w1q1 = two(quantize("w1q1", shared[0][:].bitcast(BF16)))
-        difference(diffs[0, 3], gelu_rows(0, 3, accs0[3]), ups[3])
-        for t in range(PACK):
-            g = gelu_rows(1, t, product(w1q1, t * P))
-            up = sb("up1%d" % t, [P, R], F32, "up", 2)
-            if t < 3:
-                difference(diffs[1, t], g, up)
-            else:
-                for m0 in (0, half):
-                    difference(diffs[1, t], g, up, m0, half)
-            if t in (1, 2):
-                weave_w3(t - 1, on_s, stage[t + 1])
-        w3q = two(quantize("w3q", shared[1][:].bitcast(BF16)))
+        difference(diffs[0, 3], gelu_rows(0, 3, product([w1q[0, 0], w1q[0, 1]], 3 * P, 0)), ups[3])
+        stage3 = shared[1][:].bitcast(BF16)
+        for a in range(2):
+            weave_w3(0, a, on_s, stage3[:, a * PACK * half : (a + 1) * PACK * half])
+        w3q = [two(quantize("w3q0", stage3))]
         dg = [staged("dg%d" % b) for b in range(2)]
         for t in range(PACK):
-            round_abs(0, t)
-        weave_d(0, dg[0], on_s)
-        dq = [quantize("dq0", dg[0])]
+            g = gelu_rows(1, t, product(w1q1, t * P, (6, 2, 4, 0)[t]))
+            up = sb("up1%d" % t, [P, R], F32, "up", 2)
+            difference(diffs[1, t], g, up)
+            if t == 3:
+                for tt in range(PACK):
+                    round_abs(0, tt)
+                weave_d(0, dg[0], on_s)
+                dq = [quantize("dq0", dg[0])]
         for t in range(3):
             round_abs(1, t)
         dq.append((sb("dq1c", [P, R], U32), sb("dq1s", [P, R], U8)))
@@ -263,12 +279,23 @@ def tile_list_sluice_gate_features_kernel(
             weave_d(1, dg[1], on_v, m0, half)
         for m0 in (0, half):
             quantize_cols(dq[1][0], dq[1][1], dg[1], m0, half)
-        for n in range(N // P):
-            sk = skip_rows(n, [on_s, on_s])
-            y = sb("y%d" % n, [P, R], F32)
-            if n == 0:
-                for m0 in (0, half):
-                    gated(n, sk, y, m0, half)
-            else:
-                gated(n, sk, y, 0, R)
-            finish(n, y)
+        sks = [skip_rows(0, [on_s, on_s])]
+        w3q.append(
+            [
+                quantize("w3q10", weave_w3(1, 0, on_s, dg[0][:, 0 : PACK * half])),
+                quantize("w3q11", weave_w3(1, 1, on_v, dg[1][:, PACK * half : PACK * R])),
+            ]
+        )
+        ys = [sb("y%d" % n, [P, R], F32) for n in range(N // P)]
+        for rows in ((0, 1), (2, 3)):
+            for n in rows:
+                if n > 0:
+                    sks.append(skip_rows(n, [on_s, on_s]))
+            for n in rows:
+                if n == 0:
+                    for m0 in (0, half):
+                        gated(n, sks[0], ys[n], m0, half)
+                else:
+                    gated(n, sks[n], ys[n], 0, R)
+            for n in rows:
+                finish(n, ys[n])

from contextlib import ExitStack

import concourse.mybir as mybir

F32 = mybir.dt.float32
BF16 = mybir.dt.bfloat16
I32 = mybir.dt.int32
U32 = mybir.dt.uint32
U16 = mybir.dt.uint16
U8 = mybir.dt.uint8
FP8X4 = mybir.dt.float8_e4m3fn_x4
FP4X4 = mybir.dt.float4_e2m1fn_x4
ACT = mybir.ActivationFunctionType
ALU = mybir.AluOpType

K, H, N, T, S, R, J = 1024, 1024, 512, 4096, 1024, 512, 256
FLOPS = 2 * K * H * S + 2 * K * N * S + 2 * H * N * R

P = 128
PACK = 4
PASS = P * PACK
BANK = 512
QUAD = 32


def tile_list_sluice_gate_features_kernel(
    tc, tab_words, tab_scales, offs, pos1, pos2, pos3, pos4, w1, gain, w3, w4_words, w4_scales, out
):
    nc = tc.nc
    with ExitStack() as ctx:
        keep = ctx.enter_context(tc.tile_pool(name="keep", bufs=1))
        reuse = ctx.enter_context(tc.tile_pool(name="reuse", bufs=1))
        psum = ctx.enter_context(tc.psum_pool(name="psum", bufs=1))

        def sb(name, shape, dtype, tag="", bufs=1):
            return keep.tile(shape, dtype, name=name, tag=tag or name, bufs=bufs, align_bytes=64)

        def load_list(name, src):
            lst = keep.tile(list(src.shape), U16, name=name)
            nc.sync.dma_start(lst[:], src)
            return lst

        tab_sc = sb("tab_sc", [P, T // 4], I32)
        nc.vector.memset(tab_sc[:], 0)
        for q in range(4):
            nc.gpsimd.dma_start(
                out=tab_sc[QUAD * q : QUAD * q + 8, :], in_=tab_scales[:, 4 * q : 4 * q + 4, :].bitcast(I32)
            )
        w4_sc = sb("w4_sc", [P, 2, N // 4], I32)
        nc.vector.memset(w4_sc[:], 0)


        def load_table(a):
            words = sb("tab_w%d" % a, [P, T], I32)
            nc.sync.dma_start(out=words[:], in_=tab_words[a].rearrange("p t i -> p (t i)").bitcast(I32))
            return words

        def load_weight(name, w, a, c0, width):
            raw = sb(name, [P, PACK, width], F32)
            rows = w[a * PASS : (a + 1) * PASS, c0 : c0 + width]
            nc.sync.dma_start(out=raw[:], in_=rows.rearrange("(p j) c -> p j c", j=PACK))
            return raw

        half = PASS // 2
        w1_raw = {}
        tab_w = [load_table(0)]
        idx = load_list("idx", offs)
        w1_raw[0, 0] = [load_weight("w1r00", w1, 0, 0, PASS)]
        tab_w.append(load_table(1))
        w1_raw[0, 1] = [load_weight("w1r01%d" % u, w1, 1, u * half, half) for u in range(2)]
        p1 = load_list("p1", pos1)
        p2 = load_list("p2", pos2)
        for a in range(2):
            w1_raw[1, a] = [load_weight("w1r1%d" % a, w1, a, PASS, PASS)]
        gains = sb("gains", [P, 2, PACK], F32)
        nc.sync.dma_start(out=gains[:], in_=gain.rearrange("(b p t) -> p b t", b=2, t=PACK))
        w3_raw = [load_weight("w3r%d" % a, w3, a, 0, N) for a in range(2)]
        w4_w = sb("w4_w", [P, 2, 2 * N // 4], I32)
        nc.sync.dma_start(out=w4_w[:], in_=w4_words.rearrange("a p c -> p a c").bitcast(I32))
        for q in range(4):
            nc.sync.dma_start(
                out=w4_sc[QUAD * q : QUAD * q + 4, :, :],
                in_=w4_scales[:, 4 * q : 4 * q + 4, :].rearrange("a r c -> r a c").bitcast(I32),
            )
        p3 = load_list("p3", pos3)
        p4 = load_list("p4", pos4)

        v_w = []

        def pick_words(a, tag):
            picked = sb("v_w%d" % a, [P, S], U32, tag)
            nc.vector.tensor_copy(picked[:], tab_w[a][:].bitcast(U32).indirect(idx[:]))
            v_w.append(picked)

        def quantize(name, grouped, parts=1, tag=""):
            width = grouped.shape[1] // PACK
            codes = sb(name + "c", [P, width], U32, tag)
            scales = sb(name + "s", [P, width], U8)
            step = width // parts
            for c in range(0, width, step):
                quantize_cols(codes, scales, grouped, c, step)
            return codes, scales

        def quantize_cols(codes, scales, grouped, c, step):
            nc.vector.quantize_mx(
                out=codes[:, c : c + step].bitcast(FP8X4),
                scales=scales[:, c : c + step],
                in_=grouped[:, PACK * c : PACK * (c + step)],
            )

        def weave_w1(raw, copy, grouped, t0=0, t1=PACK):
            dst = grouped[:].rearrange("p (t m j) -> p m j t", t=PACK, j=PACK)
            src = raw[:].rearrange("p j (m t) -> p m j t", t=PACK)
            copy(out=dst[:, :, :, t0:t1], in_=src[:, :, :, t0:t1])

        def weave_w3(u, a, copy, grouped):
            copy(
                out=grouped.rearrange("p (c i j) -> p c j i", i=4, j=PACK),
                in_=w3_raw[a][:, :, u * half : (u + 1) * half].rearrange("p j (c i) -> p c j i", i=4),
            )
            return grouped

        banks = []

        def table_pass(acc, weight, col, a, s0):
            codes, scales = weight
            nc.tensor.matmul_mx(
                out=acc[:],
                lhsT=codes[:, col : col + P].bitcast(FP8X4),
                lhsT_scale=scales[:, col : col + P],
                rhs=v_w[a][:, s0 : s0 + BANK].bitcast(FP8X4),
                rhs_scale=v_sc[4 * a : P, s0 : s0 + BANK],
                start=(a == 0),
                stop=(a == 1),
            )

        def bank(index):
            name = "acc%d" % len(banks)
            banks.append(psum.tile([P, BANK], F32, name=name, offset=4 * BANK * index))
            return banks[-1]

        def gelu_rows(b, t, accs):
            g = sb("g%d%d" % (b, t), [P, S], F32, "page", 6)
            for s in range(2):
                nc.scalar.activation(out=g[:, s * BANK : (s + 1) * BANK], in_=accs[s][:], func=ACT.Gelu_apprx_tanh)
            return g

        def product(weight, col, first):
            accs = [bank(first), bank(first + 1)]
            for a in range(2):
                for s in range(2):
                    table_pass(accs[s], weight[a], col, a, s * BANK)
            return accs

        def difference(diff, g, up):
            parts = [(slice(m0, m0 + half), slice(m0 // 16, (m0 + half) // 16)) for m0 in (0, half)]
            for cols, lst in parts:
                nc.vector.tensor_copy(up[:, cols], g[:].indirect(p1[:, lst]))
            for cols, lst in parts:
                nc.vector.tensor_tensor(diff[:, cols], g[:].indirect(p2[:, lst]), up[:, cols], ALU.subtract)

        def round_abs(b, t, m0=0, width=R):
            cols = slice(m0, m0 + width)
            nc.scalar.activation(
                out=d_rows[b][:, t, cols], in_=diffs[b, t][:, cols], func=ACT.Abs, scale=gains[:, b, t : t + 1]
            )

        def weave_d(b, grouped, copy, m0=0, width=R):
            copy(
                out=grouped[:, PACK * m0 : PACK * (m0 + width)].rearrange("p (c i t) -> p c t i", i=4, t=PACK),
                in_=d_rows[b][:, :, m0 : m0 + width].rearrange("p t (c i) -> p c t i", i=4),
            )

        def skip_rows(n, copies):
            accs = product(w3q[n // 2], (n % 2) * P, (6, 2)[n % 2])
            sk = sb("sk%d" % n, [P, S], F32, "page", 6)
            for s in range(2):
                copies[s](out=sk[:, s * BANK : (s + 1) * BANK], in_=accs[s][:])
            return sk

        def gated(n, sk, y, m0, width):
            cols = slice(m0, m0 + width)
            acc = bank((4 + m0 // half, 0, 6, 7)[n])
            for b in range(2):
                codes, scales = dq[b]
                nc.tensor.matmul_mx(
                    out=acc[:, 0:width],
                    lhsT=w4_w[:, b, :].bitcast(U8)[:, 2 * n * P : 2 * (n + 1) * P].bitcast(FP4X4),
                    lhsT_scale=w4_sc[:, b, :].bitcast(U8)[:, n * P : (n + 1) * P],
                    rhs=codes[:, cols].bitcast(FP8X4),
                    rhs_scale=scales[:, cols],
                    start=(b == 0),
                    stop=(b == 1),
                )
            gate = sb("gate%d_%d" % (n, m0), [P, width], F32)
            nc.scalar.activation(out=gate[:], in_=acc[:, 0:width], func=ACT.Tanh)
            lst = slice(m0 // 16, (m0 + width) // 16)
            nc.vector.tensor_tensor(y[:, cols], sk[:].indirect(p2[:, lst]), gate[:], ALU.mult)

        def finish(n, y):
            pair = sb("pair%d" % n, [P, 2, J], F32)
            nc.vector.tensor_copy(pair[:, 0, :], y[:].indirect(p3[:]))
            nc.vector.tensor_copy(pair[:, 1, :], y[:].indirect(p4[:]))
            best = sb("best%d" % n, [P, J], F32)
            nc.vector.tensor_tensor(best[:], pair[:, 0, :], pair[:, 1, :], ALU.max)
            nc.sync.dma_start(out=out[n * P : (n + 1) * P, :], in_=best[:])

        on_v, on_s = nc.vector.tensor_copy, nc.scalar.copy

        def staged(name, tag=""):
            return sb(name, [P, PACK * PASS], BF16, tag)

        def two(pair):
            codes, scales = pair
            w = codes.shape[1] // 2
            return [(codes[:, a * w : (a + 1) * w], scales[:, a * w : (a + 1) * w]) for a in range(2)]

        pick_words(0, "")
        w1q = {}
        stage00 = reuse.tile([P, PACK * PASS], BF16, name="w1g00", offset=0, align_bytes=64)
        weave_w1(w1_raw[0, 0][0], on_s, stage00, 2, 4)
        weave_w1(w1_raw[0, 0][0], on_v, stage00, 0, 2)
        w1q[0, 0] = quantize("w1q00", stage00)
        v_sc = reuse.tile([P, S], U8, name="v_sc", offset=0, align_bytes=64)
        nc.vector.tensor_copy(v_sc[:], tab_sc[:].bitcast(U8).indirect(idx[:]))
        accs0 = [[bank(2 * t + s) for s in range(2)] for t in range(3)]
        for t in range(3):
            for s in range(2):
                table_pass(accs0[t][s], w1q[0, 0], t * P, 0, s * BANK)
        pick_words(1, "")
        w1q[0, 1] = (sb("w1q01c", [P, PASS], U32), sb("w1q01s", [P, PASS], U8))
        parts = [sb("w1g01%d" % u, [P, PACK * half], BF16) for u in range(2)]
        for u in range(2):
            weave_w1(w1_raw[0, 1][u], [on_s, on_v][u], parts[u])
        for t in range(PACK):
            for u in (1, 0):
                cols = slice(t * P + u * (P // 2), t * P + (u + 1) * (P // 2))
                nc.vector.quantize_mx(
                    out=w1q[0, 1][0][:, cols].bitcast(FP8X4),
                    scales=w1q[0, 1][1][:, cols],
                    in_=parts[u][:, t * half : (t + 1) * half],
                )
        for t in range(3):
            for s in range(2):
                table_pass(accs0[t][s], w1q[0, 1], t * P, 1, s * BANK)

        d_rows = [sb("drows%d" % b, [P, PACK, R], BF16) for b in range(2)]
        diffs = {(b, t): sb("diff%d%d" % (b, t), [P, R], F32) for b in range(2) for t in range(PACK)}
        shared = [sb("shared0", [P, 4 * R], F32), sb("shared1", [P, 2 * R], F32)]
        ups = [sb("up0%d" % t, [P, R], F32, "up", 2) for t in range(PACK)]
        ups[0] = shared[0][:, 3 * half : 5 * half]
        ups[2] = shared[1][:, half : 3 * half]
        gs = [gelu_rows(0, t, accs0[t]) for t in range(3)]
        for t in range(3):
            difference(diffs[0, t], gs[t], ups[t])
        for a in range(2):
            weave_w1(w1_raw[1, a][0], on_s, shared[0][:, 2 * R * a : 2 * R * (a + 1)].bitcast(BF16))
        w1q1 = two(quantize("w1q1", shared[0][:].bitcast(BF16)))
        difference(diffs[0, 3], gelu_rows(0, 3, product([w1q[0, 0], w1q[0, 1]], 3 * P, 0)), ups[3])
        stage3 = shared[1][:].bitcast(BF16)
        for a in range(2):
            weave_w3(0, a, on_s, stage3[:, a * PACK * half : (a + 1) * PACK * half])
        w3q = [two(quantize("w3q0", stage3))]
        dg = [staged("dg%d" % b) for b in range(2)]
        for t in range(PACK):
            g = gelu_rows(1, t, product(w1q1, t * P, (6, 2, 4, 0)[t]))
            up = sb("up1%d" % t, [P, R], F32, "up", 2)
            difference(diffs[1, t], g, up)
            if t == 3:
                for tt in range(PACK):
                    round_abs(0, tt)
                weave_d(0, dg[0], on_s)
                dq = [quantize("dq0", dg[0])]
        for t in range(3):
            round_abs(1, t)
        dq.append((sb("dq1c", [P, R], U32), sb("dq1s", [P, R], U8)))
        for m0 in (0, half):
            round_abs(1, 3, m0, half)
            weave_d(1, dg[1], on_v, m0, half)
        for m0 in (0, half):
            quantize_cols(dq[1][0], dq[1][1], dg[1], m0, half)
        sks = [skip_rows(0, [on_s, on_s])]
        w3q.append(
            [
                quantize("w3q10", weave_w3(1, 0, on_s, dg[0][:, 0 : PACK * half])),
                quantize("w3q11", weave_w3(1, 1, on_v, dg[1][:, PACK * half : PACK * R])),
            ]
        )
        ys = [sb("y%d" % n, [P, R], F32) for n in range(N // P)]
        for rows in ((0, 1), (2, 3)):
            for n in rows:
                if n > 0:
                    sks.append(skip_rows(n, [on_s, on_s]))
            for n in rows:
                if n == 0:
                    for m0 in (0, half):
                        gated(n, sks[0], ys[n], m0, half)
                else:
                    gated(n, sks[n], ys[n], 0, R)
            for n in rows:
                finish(n, ys[n])
